import numpy as np
import ml_dtypes


def mxq(x, axis, fmt="e4m3"):
    dtype, down = {"e4m3": (ml_dtypes.float8_e4m3fn, 7), "e5m2": (ml_dtypes.float8_e5m2, 14)}[fmt]
    v = np.moveaxis(np.asarray(x, np.float32).astype(ml_dtypes.bfloat16).astype(np.float64), axis, -1)
    blocks = v.reshape(v.shape[:-1] + (-1, 32))
    amax = np.abs(blocks).max(-1, keepdims=True)
    byte = np.maximum(np.where(amax > 0, np.frexp(amax)[1] - 1 + 127, 0) - down, 1)
    scale = np.exp2(byte - 127.0)
    codes = (blocks / scale).astype(np.float32).astype(dtype).astype(np.float64)
    return np.moveaxis((codes * scale).reshape(v.shape), -1, axis)


WIDE = False


def mx_kscale(k):
    if not WIDE:
        return np.ones(k)
    levels = np.array([10, -10, 5, -5, 0])
    if k % 512:
        return np.exp2(np.random.permutation(np.resize(levels, k // 32))).repeat(32)
    a = np.empty((k // 512, 16))
    for p in range(k // 512):
        a[p, :8] = np.random.permutation(np.resize(levels, 8))
        for g in range(8):
            far = levels[np.abs(levels - a[p, g]) >= 10]
            a[p, g + 8] = far[np.random.randint(len(far))]
    return np.exp2(a.ravel()).repeat(32)


def f64(x):
    return np.asarray(x).astype(np.float64)


def striped(idx):
    return np.tile(idx.reshape(-1, 16).T, (8, 1)).astype(np.uint16)


def unstriped(offs):
    return offs[:16].T.reshape(-1).astype(np.int64)


def pack_weight(w):
    k, n = w.shape
    w = f64(np.asarray(w, np.float32).astype(ml_dtypes.bfloat16)).reshape(k // 32, 32, n)
    amax = np.abs(w).max(1)
    byte = np.clip(np.where(amax > 0, np.frexp(amax)[1] - 1 + 127 - 7, 1), 1, 254)
    scaled = (w * np.exp2(127.0 - byte)[:, None, :]).reshape(k, n).astype(np.float32)
    words = np.ascontiguousarray(scaled.reshape(k // 512, 128, 4, n).transpose(0, 1, 3, 2)).astype(ml_dtypes.float8_e4m3fn).view(np.uint8)
    return words, np.ascontiguousarray(byte.astype(np.uint8).reshape(k // 512, 16, n))


def unpack_weight(words, scales):
    g, p, n, _ = words.shape
    vals = np.ascontiguousarray(words).view(ml_dtypes.float8_e4m3fn).astype(np.float64) * np.repeat(np.exp2(scales.astype(np.float64) - 127.0), 8, axis=1)[..., None]
    return vals.transpose(0, 1, 3, 2).reshape(g * 512, n)


K, T, S, D, N = 512, 4096, 1024, 4, 128
P = 2 ** 7


def setup_inputs():
    n = np.random.standard_normal
    s = mx_kscale(K)[:, None]
    packed_xT = pack_weight(n((K, T)) * s)
    return {
        "x_words": packed_xT[0],
        "x_scales": packed_xT[1],
        "w1": (n((K, N)) / np.sqrt(K) / s).astype(np.float32),
        "w2": (n((K, N)) / np.sqrt(K) / s).astype(np.float32),
        "w3": (n((K, N)) / np.sqrt(K) / s).astype(np.float32),
        "vis": (np.tile(np.random.uniform(0.0, 1.0, S), (P, 1))).astype(np.float32),
        "kap": (np.random.uniform(0.2, 0.8, (N, 1))).astype(np.float32),
        "offs": striped(np.random.permutation(T)[:S]),
    }


def reference(x_words, x_scales, w1, w2, w3, vis, kap, offs):
    xq = unpack_weight(x_words, x_scales)[:, unstriped(offs)]
    yp = mxq(f64(w2), 0, "e4m3").T @ xq
    pdfa = np.log(np.exp(yp) + 1.0) + 0.2
    yq = mxq(f64(w3), 0, "e4m3").T @ xq
    pdfb = np.log(np.exp(yq) + 1.0) + 0.2
    wt = pdfa / (pdfa + pdfb)
    yf = mxq(f64(w1), 0, "e4m3").T @ xq
    con = np.exp(0.6 * yf)
    est = (f64(vis)[:1] * wt) * (con / pdfa)
    mean = est.reshape(len(est), -1, D).mean(axis=2)
    dv = (est - np.repeat(mean, D, axis=1)) ** 2
    return mean + f64(kap) * (np.sqrt(dv.reshape(len(dv), -1, D).mean(axis=2) + 0.05))

@@ -1,0 +1,182 @@
+import math
+from contextlib import ExitStack
+
+import concourse.mybir as mybir
+
+K, T, S, D, N = 512, 4096, 1024, 4, 128
+FLOPS = 3 * 2 * K * N * S
+
+F32 = mybir.dt.float32
+BF16 = mybir.dt.bfloat16
+I32 = mybir.dt.int32
+U32 = mybir.dt.uint32
+U16 = mybir.dt.uint16
+U8 = mybir.dt.uint8
+FP8X4 = mybir.dt.float8_e4m3fn_x4
+ALU = mybir.AluOpType
+ACT = mybir.ActivationFunctionType
+
+P = 128
+PACK = 4
+HALVES = 2
+HALF = S // HALVES
+PIECES = ((0, 64), (64, 192), (192, 256))
+FLOOR = 2.0 ** -30
+KNEE = math.log(1.0 / FLOOR - 1.0)
+
+
+def tile_picked_ymisw_bal_p_kernel(tc, x_words, x_scales, w1, w2, w3, vis, kap, offs, out):
+    nc = tc.nc
+    with ExitStack() as ctx:
+        keep = ctx.enter_context(tc.tile_pool(name="keep", bufs=1))
+        psum = ctx.enter_context(tc.psum_pool(name="psum", bufs=1))
+
+        def tile(name, shape, dtype):
+            return keep.tile(shape, dtype, name=name, align_bytes=64)
+
+        def per_half(name, width):
+            return [tile("%s%d" % (name, h), [P, width], F32) for h in range(HALVES)]
+
+        offsets = keep.tile([P, S // 16], U16, name="offsets")
+        nc.sync.dma_start(offsets[:], offs)
+
+        seed = tile("seed", [P, 1], F32)
+        warm = tile("warm", [P, 1], F32)
+        nc.gpsimd.memset(seed[:], 0.0)
+        nc.scalar.activation(warm[:], seed[:], ACT.Sigmoid)
+
+        scale_table = tile("scale_table", [P, T], U8)
+        nc.vector.memset(scale_table[:].bitcast(I32), 0)
+        raw = {}
+
+        def load_weight(name, w, slot):
+            raw[name] = keep.tile([P, PACK, N], F32, name="raw_" + name, tag="raw_" + slot)
+            nc.sync.dma_start(raw[name][:], w.rearrange("(p j) n -> p j n", j=PACK))
+
+        load_weight("p", w2, "first")
+        load_weight("q", w3, "second")
+        for q in range(4):
+            nc.sync.dma_start(
+                scale_table[32 * q : 32 * q + 4, :].bitcast(I32),
+                x_scales[0, 4 * q : 4 * q + 4, :].bitcast(I32),
+            )
+        word_table = tile("word_table", [P, T], I32)
+        nc.sync.dma_start(word_table[:], x_words[0].rearrange("p n t -> p (n t)").bitcast(I32))
+
+        codes, scales = {}, {}
+
+        def quantize_weight(name):
+            grouped = tile("grouped_" + name, [P, N * PACK], BF16)
+            nc.scalar.copy(
+                grouped[:].rearrange("p (c i j) -> p c j i", i=4, j=PACK),
+                raw[name][:].rearrange("p j (c i) -> p c j i", i=4),
+            )
+            codes[name] = tile("codes_" + name, [P, N], U32)
+            scales[name] = tile("scales_" + name, [P, N], U8)
+            nc.vector.quantize_mx(out=codes[name][:].bitcast(FP8X4), scales=scales[name][:], in_=grouped[:])
+
+        picked_scales = tile("picked_scales", [P, S], U8)
+        nc.vector.tensor_copy(picked_scales[:], scale_table[:].indirect(offsets[:]))
+        quantize_weight("p")
+        quantize_weight("q")
+
+        load_weight("f", w1, "first")
+        vis_sb = keep.tile([P, S], F32, name="vis_sb", tag="raw_second")
+        nc.sync.dma_start(vis_sb[:], vis)
+        kap_sb = tile("kap_sb", [P, 1], F32)
+        nc.sync.dma_start(kap_sb[:], kap)
+
+        picked_words = [tile("picked_words%d" % h, [P, HALF], U32) for h in range(HALVES)]
+        cols = HALF // 16
+        for h in range(HALVES):
+            nc.vector.tensor_copy(
+                picked_words[h][:],
+                word_table[:].bitcast(U32).indirect(offsets[:, h * cols : (h + 1) * cols]),
+            )
+
+        y = {}
+
+        def product(name, h):
+            y[name, h] = psum.tile([P, HALF], F32, name="y_%s%d" % (name, h))
+            nc.tensor.matmul_mx(
+                out=y[name, h][:],
+                lhsT=codes[name][:].bitcast(FP8X4),
+                lhsT_scale=scales[name][:],
+                rhs=picked_words[h][:].bitcast(FP8X4),
+                rhs_scale=picked_scales[:, h * HALF : (h + 1) * HALF],
+                start=True,
+                stop=True,
+            )
+
+        sig_p, sig_q = per_half("sig_p", HALF), per_half("sig_q", HALF)
+        for h in range(HALVES):
+            product("p", h)
+            product("q", h)
+            nc.scalar.activation(sig_p[h][:], y["p", h][:], ACT.Sigmoid, scale=-1.0)
+            nc.scalar.activation(sig_q[h][:], y["q", h][:], ACT.Sigmoid, scale=-1.0)
+
+        log_joint = per_half("log_joint", HALF)
+        nc.scalar.activation(log_joint[0][:, 0:1], sig_q[1][:, 0:1], ACT.Ln)
+
+        over_p, over = per_half("over_p", HALF), per_half("over", HALF)
+        floor_q, joint = per_half("floor_q", HALF), per_half("joint", HALF)
+
+        def excess(h):
+            nc.vector.tensor_scalar(over_p[h][:], y["p", h][:], KNEE, -2.0 * KNEE, ALU.max, ALU.add)
+            nc.vector.scalar_tensor_tensor(over[h][:], y["q", h][:], KNEE, over_p[h][:], ALU.max, ALU.add)
+
+        excess(0)
+        for h in range(HALVES):
+            nc.vector.tensor_scalar_max(floor_q[h][:], sig_q[h][:], FLOOR)
+            nc.vector.scalar_tensor_tensor(joint[h][:], sig_p[h][:], FLOOR, floor_q[h][:], ALU.max, ALU.mult)
+        excess(1)
+
+        for h in range(HALVES):
+            nc.scalar.activation(log_joint[h][:], joint[h][:], ACT.Ln)
+
+        density, log_density = per_half("density", HALF), per_half("log_density", HALF)
+        for h in range(HALVES):
+            nc.vector.scalar_tensor_tensor(density[h][:], over[h][:], 0.4, log_joint[h][:], ALU.add, ALU.subtract)
+            nc.scalar.activation(log_density[h][:], density[h][:], ACT.Ln, scale=float(D))
+
+        quantize_weight("f")
+        for h in range(HALVES):
+            product("f", h)
+
+        ratio = tile("ratio", [P, S], F32)
+        nc.scalar.activation(ratio[:, 0:1], log_density[1][:, 0:1], ACT.Exp)
+        expo = tile("expo", [P, S], F32)
+        for h in range(HALVES):
+            nc.vector.scalar_tensor_tensor(
+                expo[:, h * HALF : (h + 1) * HALF], y["f", h][:], 0.6, log_density[h][:], ALU.mult, ALU.subtract
+            )
+        for lo, hi in PIECES:
+            nc.scalar.activation(ratio[:, D * lo : D * hi], expo[:, D * lo : D * hi], ACT.Exp)
+
+        def per_piece(name, factor):
+            return [tile("%s%d" % (name, i), [P, factor * (hi - lo)], F32) for i, (lo, hi) in enumerate(PIECES)]
+
+        squares = per_piece("squares", 3)
+        nc.scalar.activation(squares[0][:, 0:1], ratio[:, S - 1 : S], ACT.Sqrt)
+
+        est, pair_sum, diffs = per_piece("est", 4), per_piece("pair_sum", 2), per_piece("diffs", 3)
+        mean, inner, variance = per_piece("mean", 1), per_piece("inner", 1), per_piece("variance", 1)
+        spread, result = per_piece("spread", 1), per_piece("result", 1)
+        for i, (lo, hi) in enumerate(PIECES):
+            n = hi - lo
+            nc.vector.tensor_tensor(est[i][:], ratio[:, D * lo : D * hi], vis_sb[:, D * lo : D * hi], ALU.mult)
+            nc.vector.tensor_tensor(pair_sum[i][:], est[i][:, 0::2], est[i][:, 1::2], ALU.add)
+            nc.vector.tensor_tensor(diffs[i][:, : 2 * n], est[i][:, 0::2], est[i][:, 1::2], ALU.subtract)
+            nc.vector.tensor_tensor(diffs[i][:, 2 * n :], pair_sum[i][:, 0::2], pair_sum[i][:, 1::2], ALU.subtract)
+            nc.scalar.activation(squares[i][:], diffs[i][:], ACT.Square)
+
+        for i, (lo, hi) in enumerate(PIECES):
+            n = hi - lo
+            nc.vector.tensor_tensor(inner[i][:], squares[i][:, 0 : 2 * n : 2], squares[i][:, 1 : 2 * n : 2], ALU.add)
+            nc.vector.tensor_tensor(mean[i][:], pair_sum[i][:, 0::2], pair_sum[i][:, 1::2], ALU.add)
+            nc.vector.scalar_tensor_tensor(variance[i][:], inner[i][:], 2.0, squares[i][:, 2 * n :], ALU.mult, ALU.add)
+            nc.scalar.activation(spread[i][:], variance[i][:], ACT.Sqrt, bias=0.05)
+
+        for i, (lo, hi) in enumerate(PIECES):
+            nc.vector.scalar_tensor_tensor(result[i][:], spread[i][:], kap_sb[:, 0:1], mean[i][:], ALU.mult, ALU.add)
+            nc.sync.dma_start(out[:, lo:hi], result[i][:])

@@ -20,6 +20,7 @@ P = 128
 PACK = 4
 HALVES = 2
 HALF = S // HALVES
+QUARTER = S // 4
 PIECES = ((0, 64), (64, 192), (192, 256))
 FLOOR = 2.0 ** -30
 KNEE = math.log(1.0 / FLOOR - 1.0)
@@ -31,60 +32,62 @@ def tile_picked_ymisw_bal_p_kernel(tc, x_words, x_scales, w1, w2, w3, vis, kap, 
         keep = ctx.enter_context(tc.tile_pool(name="keep", bufs=1))
         psum = ctx.enter_context(tc.psum_pool(name="psum", bufs=1))
 
-        def tile(name, shape, dtype):
-            return keep.tile(shape, dtype, name=name, align_bytes=64)
-
-        def per_half(name, width):
-            return [tile("%s%d" % (name, h), [P, width], F32) for h in range(HALVES)]
+        def tile(name, shape, dtype, tag=None):
+            return keep.tile(shape, dtype, name=name, tag=tag or name, align_bytes=64)
 
         offsets = keep.tile([P, S // 16], U16, name="offsets")
         nc.sync.dma_start(offsets[:], offs)
 
-        seed = tile("seed", [P, 1], F32)
-        warm = tile("warm", [P, 1], F32)
-        nc.gpsimd.memset(seed[:], 0.0)
-        nc.scalar.activation(warm[:], seed[:], ACT.Sigmoid)
-
         scale_table = tile("scale_table", [P, T], U8)
         nc.vector.memset(scale_table[:].bitcast(I32), 0)
+
+        seed = tile("seed", [P, 1], F32)
+        warm = tile("warm", [P, 1], F32)
+        nc.vector.memset(seed[:], 0.0)
+        nc.scalar.activation(warm[:], seed[:], ACT.Sigmoid)
+
+        planes = tile("planes", [P, S], U8)
+        nc.vector.memset(planes[:].bitcast(I32), 0)
+
         raw = {}
 
-        def load_weight(name, w, slot):
-            raw[name] = keep.tile([P, PACK, N], F32, name="raw_" + name, tag="raw_" + slot)
+        def load_weight(name, w):
+            raw[name] = tile("raw_" + name, [P, PACK, N], F32)
             nc.sync.dma_start(raw[name][:], w.rearrange("(p j) n -> p j n", j=PACK))
 
-        load_weight("p", w2, "first")
-        load_weight("q", w3, "second")
-        for q in range(4):
-            nc.sync.dma_start(
-                scale_table[32 * q : 32 * q + 4, :].bitcast(I32),
-                x_scales[0, 4 * q : 4 * q + 4, :].bitcast(I32),
-            )
+        kap_sb = tile("kap_sb", [P, 1], F32)
+        nc.sync.dma_start(kap_sb[:], kap)
+        load_weight("p", w2)
+        load_weight("q", w3)
+        nc.sync.dma_start(scale_table[0:P:8, :].bitcast(I32), x_scales[0].bitcast(I32))
         word_table = tile("word_table", [P, T], I32)
         nc.sync.dma_start(word_table[:], x_words[0].rearrange("p n t -> p (n t)").bitcast(I32))
+        load_weight("f", w1)
 
-        codes, scales = {}, {}
+        grouped, codes, scales = {}, {}, {}
 
-        def quantize_weight(name):
-            grouped = tile("grouped_" + name, [P, N * PACK], BF16)
+        def round_weight(name):
+            grouped[name] = tile("grouped_" + name, [P, N * PACK], BF16)
             nc.scalar.copy(
-                grouped[:].rearrange("p (c i j) -> p c j i", i=4, j=PACK),
+                grouped[name][:].rearrange("p (c i j) -> p c j i", i=4, j=PACK),
                 raw[name][:].rearrange("p j (c i) -> p c j i", i=4),
             )
-            codes[name] = tile("codes_" + name, [P, N], U32)
+
+        def quantize_weight(name, tag=None):
+            codes[name] = tile("codes_" + name, [P, N], U32, tag)
             scales[name] = tile("scales_" + name, [P, N], U8)
-            nc.vector.quantize_mx(out=codes[name][:].bitcast(FP8X4), scales=scales[name][:], in_=grouped[:])
+            nc.vector.quantize_mx(out=codes[name][:].bitcast(FP8X4), scales=scales[name][:], in_=grouped[name][:])
 
         picked_scales = tile("picked_scales", [P, S], U8)
         nc.vector.tensor_copy(picked_scales[:], scale_table[:].indirect(offsets[:]))
-        quantize_weight("p")
-        quantize_weight("q")
-
-        load_weight("f", w1, "first")
-        vis_sb = keep.tile([P, S], F32, name="vis_sb", tag="raw_second")
+        for j in range(4):
+            nc.scalar.dma_start(planes[j:P:32, :].bitcast(I32), picked_scales[8 * j : P : 32, :].bitcast(I32))
+        vis_sb = tile("vis_sb", [P, S], F32, "picked_scales")
         nc.sync.dma_start(vis_sb[:], vis)
-        kap_sb = tile("kap_sb", [P, 1], F32)
-        nc.sync.dma_start(kap_sb[:], kap)
+        for name in ("p", "q"):
+            round_weight(name)
+            quantize_weight(name)
+        round_weight("f")
 
         picked_words = [tile("picked_words%d" % h, [P, HALF], U32) for h in range(HALVES)]
         cols = HALF // 16
@@ -103,52 +106,61 @@ def tile_picked_ymisw_bal_p_kernel(tc, x_words, x_scales, w1, w2, w3, vis, kap, 
                 lhsT=codes[name][:].bitcast(FP8X4),
                 lhsT_scale=scales[name][:],
                 rhs=picked_words[h][:].bitcast(FP8X4),
-                rhs_scale=picked_scales[:, h * HALF : (h + 1) * HALF],
+                rhs_scale=planes[:, h * HALF : (h + 1) * HALF],
                 start=True,
                 stop=True,
             )
 
-        sig_p, sig_q = per_half("sig_p", HALF), per_half("sig_q", HALF)
+        halves = [slice(h * HALF, (h + 1) * HALF) for h in range(HALVES)]
+        quarters = [slice(a, a + QUARTER) for a in range(0, S, QUARTER)]
+
+        sig = tile("sig", [P, 2 * S], F32)
+        sig_p, sig_q = sig[:, :S], sig[:, S:]
         for h in range(HALVES):
             product("p", h)
             product("q", h)
-            nc.scalar.activation(sig_p[h][:], y["p", h][:], ACT.Sigmoid, scale=-1.0)
-            nc.scalar.activation(sig_q[h][:], y["q", h][:], ACT.Sigmoid, scale=-1.0)
+            nc.scalar.activation(sig_p[:, halves[h]], y["p", h][:], ACT.Sigmoid, scale=-1.0)
+            nc.scalar.activation(sig_q[:, halves[h]], y["q", h][:], ACT.Sigmoid, scale=-1.0)
 
-        log_joint = per_half("log_joint", HALF)
-        nc.scalar.activation(log_joint[0][:, 0:1], sig_q[1][:, 0:1], ACT.Ln)
+        log_joint = tile("log_joint", [P, S], F32)
+        nc.scalar.activation(log_joint[:, 0:S:QUARTER], sig[:, 0 : 2 * S : HALF], ACT.Ln)
 
-        over_p, over = per_half("over_p", HALF), per_half("over", HALF)
-        floor_q, joint = per_half("floor_q", HALF), per_half("joint", HALF)
+        over_p, over = tile("over_p", [P, S], F32), tile("over", [P, S], F32)
+        floor_q, joint = tile("floor_q", [P, S], F32), tile("joint", [P, S], F32)
 
         def excess(h):
-            nc.vector.tensor_scalar(over_p[h][:], y["p", h][:], KNEE, -2.0 * KNEE, ALU.max, ALU.add)
-            nc.vector.scalar_tensor_tensor(over[h][:], y["q", h][:], KNEE, over_p[h][:], ALU.max, ALU.add)
+            nc.vector.tensor_scalar(over_p[:, halves[h]], y["p", h][:], KNEE, -2.0 * KNEE, ALU.max, ALU.add)
+            nc.vector.scalar_tensor_tensor(over[:, halves[h]], y["q", h][:], KNEE, over_p[:, halves[h]], ALU.max, ALU.add)
+
+        def floored_product(h):
+            nc.vector.tensor_scalar_max(floor_q[:, halves[h]], sig_q[:, halves[h]], FLOOR)
+            nc.vector.scalar_tensor_tensor(
+                joint[:, halves[h]], sig_p[:, halves[h]], FLOOR, floor_q[:, halves[h]], ALU.max, ALU.mult
+            )
 
         excess(0)
-        for h in range(HALVES):
-            nc.vector.tensor_scalar_max(floor_q[h][:], sig_q[h][:], FLOOR)
-            nc.vector.scalar_tensor_tensor(joint[h][:], sig_p[h][:], FLOOR, floor_q[h][:], ALU.max, ALU.mult)
+        floored_product(0)
+        floored_product(1)
         excess(1)
 
-        for h in range(HALVES):
-            nc.scalar.activation(log_joint[h][:], joint[h][:], ACT.Ln)
+        for c in quarters:
+            nc.scalar.activation(log_joint[:, c], joint[:, c], ACT.Ln)
 
-        density, log_density = per_half("density", HALF), per_half("log_density", HALF)
-        for h in range(HALVES):
-            nc.vector.scalar_tensor_tensor(density[h][:], over[h][:], 0.4, log_joint[h][:], ALU.add, ALU.subtract)
-            nc.scalar.activation(log_density[h][:], density[h][:], ACT.Ln, scale=float(D))
+        density, log_density = tile("density", [P, S], F32), tile("log_density", [P, S], F32)
+        for c in quarters:
+            nc.vector.scalar_tensor_tensor(density[:, c], over[:, c], 0.4, log_joint[:, c], ALU.add, ALU.subtract)
+            nc.scalar.activation(log_density[:, c], density[:, c], ACT.Ln, scale=float(D))
 
         quantize_weight("f")
         for h in range(HALVES):
             product("f", h)
 
         ratio = tile("ratio", [P, S], F32)
-        nc.scalar.activation(ratio[:, 0:1], log_density[1][:, 0:1], ACT.Exp)
+        nc.scalar.activation(ratio[:, 0:S:QUARTER], log_density[:, 0:S:QUARTER], ACT.Exp)
         expo = tile("expo", [P, S], F32)
         for h in range(HALVES):
             nc.vector.scalar_tensor_tensor(
-                expo[:, h * HALF : (h + 1) * HALF], y["f", h][:], 0.6, log_density[h][:], ALU.mult, ALU.subtract
+                expo[:, halves[h]], y["f", h][:], 0.6, log_density[:, halves[h]], ALU.mult, ALU.subtract
             )
         for lo, hi in PIECES:
             nc.scalar.activation(ratio[:, D * lo : D * hi], expo[:, D * lo : D * hi], ACT.Exp)
@@ -157,26 +169,39 @@ def tile_picked_ymisw_bal_p_kernel(tc, x_words, x_scales, w1, w2, w3, vis, kap, 
             return [tile("%s%d" % (name, i), [P, factor * (hi - lo)], F32) for i, (lo, hi) in enumerate(PIECES)]
 
         squares = per_piece("squares", 3)
-        nc.scalar.activation(squares[0][:, 0:1], ratio[:, S - 1 : S], ACT.Sqrt)
+        nc.scalar.activation(squares[0][:, 0:4], ratio[:, 0:S:QUARTER], ACT.Sqrt)
 
         est, pair_sum, diffs = per_piece("est", 4), per_piece("pair_sum", 2), per_piece("diffs", 3)
         mean, inner, variance = per_piece("mean", 1), per_piece("inner", 1), per_piece("variance", 1)
         spread, result = per_piece("spread", 1), per_piece("result", 1)
-        for i, (lo, hi) in enumerate(PIECES):
-            n = hi - lo
+        width = [hi - lo for lo, hi in PIECES]
+
+        def estimate(i):
+            lo, hi = PIECES[i]
             nc.vector.tensor_tensor(est[i][:], ratio[:, D * lo : D * hi], vis_sb[:, D * lo : D * hi], ALU.mult)
+
+        def within_pairs(i):
             nc.vector.tensor_tensor(pair_sum[i][:], est[i][:, 0::2], est[i][:, 1::2], ALU.add)
-            nc.vector.tensor_tensor(diffs[i][:, : 2 * n], est[i][:, 0::2], est[i][:, 1::2], ALU.subtract)
-            nc.vector.tensor_tensor(diffs[i][:, 2 * n :], pair_sum[i][:, 0::2], pair_sum[i][:, 1::2], ALU.subtract)
+            nc.vector.tensor_tensor(diffs[i][:, : 2 * width[i]], est[i][:, 0::2], est[i][:, 1::2], ALU.subtract)
+
+        def between_pairs(i):
+            nc.vector.tensor_tensor(diffs[i][:, 2 * width[i] :], pair_sum[i][:, 0::2], pair_sum[i][:, 1::2], ALU.subtract)
             nc.scalar.activation(squares[i][:], diffs[i][:], ACT.Square)
 
-        for i, (lo, hi) in enumerate(PIECES):
-            n = hi - lo
-            nc.vector.tensor_tensor(inner[i][:], squares[i][:, 0 : 2 * n : 2], squares[i][:, 1 : 2 * n : 2], ALU.add)
+        pieces = range(len(PIECES))
+        estimate(0)
+        for i in pieces:
+            within_pairs(i)
+            if i + 1 in pieces:
+                estimate(i + 1)
+            between_pairs(i)
+        for i in pieces:
             nc.vector.tensor_tensor(mean[i][:], pair_sum[i][:, 0::2], pair_sum[i][:, 1::2], ALU.add)
+        for i in pieces:
+            n = width[i]
+            nc.vector.tensor_tensor(inner[i][:], squares[i][:, 0 : 2 * n : 2], squares[i][:, 1 : 2 * n : 2], ALU.add)
             nc.vector.scalar_tensor_tensor(variance[i][:], inner[i][:], 2.0, squares[i][:, 2 * n :], ALU.mult, ALU.add)
             nc.scalar.activation(spread[i][:], variance[i][:], ACT.Sqrt, bias=0.05)
-
         for i, (lo, hi) in enumerate(PIECES):
             nc.vector.scalar_tensor_tensor(result[i][:], spread[i][:], kap_sb[:, 0:1], mean[i][:], ALU.mult, ALU.add)
             nc.sync.dma_start(out[:, lo:hi], result[i][:])

@@ -21,7 +21,7 @@ PACK = 4
 HALVES = 2
 HALF = S // HALVES
 QUARTER = S // 4
-PIECES = ((0, 64), (64, 192), (192, 256))
+PIECES = ((0, 64), (64, 128), (128, 256))
 FLOOR = 2.0 ** -30
 KNEE = math.log(1.0 / FLOOR - 1.0)
 
@@ -55,14 +55,14 @@ def tile_picked_ymisw_bal_p_kernel(tc, x_words, x_scales, w1, w2, w3, vis, kap, 
             raw[name] = tile("raw_" + name, [P, PACK, N], F32)
             nc.sync.dma_start(raw[name][:], w.rearrange("(p j) n -> p j n", j=PACK))
 
-        kap_sb = tile("kap_sb", [P, 1], F32)
-        nc.sync.dma_start(kap_sb[:], kap)
         load_weight("p", w2)
         load_weight("q", w3)
         nc.sync.dma_start(scale_table[0:P:8, :].bitcast(I32), x_scales[0].bitcast(I32))
         word_table = tile("word_table", [P, T], I32)
         nc.sync.dma_start(word_table[:], x_words[0].rearrange("p n t -> p (n t)").bitcast(I32))
         load_weight("f", w1)
+        kap_sb = tile("kap_sb", [P, 1], F32)
+        nc.sync.dma_start(kap_sb[:], kap)
 
         grouped, codes, scales = {}, {}, {}
 
@@ -97,40 +97,44 @@ def tile_picked_ymisw_bal_p_kernel(tc, x_words, x_scales, w1, w2, w3, vis, kap, 
                 word_table[:].bitcast(U32).indirect(offsets[:, h * cols : (h + 1) * cols]),
             )
 
+        halves = [slice(h * HALF, (h + 1) * HALF) for h in range(HALVES)]
+        quarters = [slice(a, a + QUARTER) for a in range(0, S, QUARTER)]
         y = {}
 
-        def product(name, h):
-            y[name, h] = psum.tile([P, HALF], F32, name="y_%s%d" % (name, h))
+        def product(name, c, bank):
+            h, lo = divmod(c.start, HALF)
+            width = c.stop - c.start
+            y[name, c.start] = psum.tile([P, width], F32, name="y_%s%d" % (name, c.start), tag="bank%d" % bank)
             nc.tensor.matmul_mx(
-                out=y[name, h][:],
+                out=y[name, c.start][:],
                 lhsT=codes[name][:].bitcast(FP8X4),
                 lhsT_scale=scales[name][:],
-                rhs=picked_words[h][:].bitcast(FP8X4),
-                rhs_scale=planes[:, h * HALF : (h + 1) * HALF],
+                rhs=picked_words[h][:, lo : lo + width].bitcast(FP8X4),
+                rhs_scale=planes[:, c],
                 start=True,
                 stop=True,
             )
 
-        halves = [slice(h * HALF, (h + 1) * HALF) for h in range(HALVES)]
-        quarters = [slice(a, a + QUARTER) for a in range(0, S, QUARTER)]
-
         sig = tile("sig", [P, 2 * S], F32)
         sig_p, sig_q = sig[:, :S], sig[:, S:]
         for h in range(HALVES):
-            product("p", h)
-            product("q", h)
-            nc.scalar.activation(sig_p[:, halves[h]], y["p", h][:], ACT.Sigmoid, scale=-1.0)
-            nc.scalar.activation(sig_q[:, halves[h]], y["q", h][:], ACT.Sigmoid, scale=-1.0)
+            for name, dst, base in (("p", sig_p, 0), ("q", sig_q, 4)):
+                for i in (2 * h, 2 * h + 1):
+                    c = quarters[i]
+                    product(name, c, base + i)
+                    nc.scalar.activation(dst[:, c], y[name, c.start][:], ACT.Sigmoid, scale=-1.0)
 
         log_joint = tile("log_joint", [P, S], F32)
-        nc.scalar.activation(log_joint[:, 0:S:QUARTER], sig[:, 0 : 2 * S : HALF], ACT.Ln)
+        nc.scalar.activation(warm[:], sig_p[:, S - 1 : S], ACT.Ln)
 
         over_p, over = tile("over_p", [P, S], F32), tile("over", [P, S], F32)
         floor_q, joint = tile("floor_q", [P, S], F32), tile("joint", [P, S], F32)
 
         def excess(h):
-            nc.vector.tensor_scalar(over_p[:, halves[h]], y["p", h][:], KNEE, -2.0 * KNEE, ALU.max, ALU.add)
-            nc.vector.scalar_tensor_tensor(over[:, halves[h]], y["q", h][:], KNEE, over_p[:, halves[h]], ALU.max, ALU.add)
+            for c in quarters[2 * h : 2 * h + 2]:
+                nc.vector.tensor_scalar(over_p[:, c], y["p", c.start][:], KNEE, -2.0 * KNEE, ALU.max, ALU.add)
+            for c in quarters[2 * h : 2 * h + 2]:
+                nc.vector.scalar_tensor_tensor(over[:, c], y["q", c.start][:], KNEE, over_p[:, c], ALU.max, ALU.add)
 
         def floored_product(h):
             nc.vector.tensor_scalar_max(floor_q[:, halves[h]], sig_q[:, halves[h]], FLOOR)
@@ -153,55 +157,61 @@ def tile_picked_ymisw_bal_p_kernel(tc, x_words, x_scales, w1, w2, w3, vis, kap, 
 
         quantize_weight("f")
         for h in range(HALVES):
-            product("f", h)
+            product("f", halves[h], h)
 
         ratio = tile("ratio", [P, S], F32)
-        nc.scalar.activation(ratio[:, 0:S:QUARTER], log_density[:, 0:S:QUARTER], ACT.Exp)
+        nc.scalar.activation(warm[:], log_density[:, HALF : HALF + 1], ACT.Exp)
         expo = tile("expo", [P, S], F32)
         for h in range(HALVES):
             nc.vector.scalar_tensor_tensor(
-                expo[:, halves[h]], y["f", h][:], 0.6, log_density[:, halves[h]], ALU.mult, ALU.subtract
+                expo[:, halves[h]], y["f", h * HALF][:], 0.6, log_density[:, halves[h]], ALU.mult, ALU.subtract
             )
         for lo, hi in PIECES:
             nc.scalar.activation(ratio[:, D * lo : D * hi], expo[:, D * lo : D * hi], ACT.Exp)
 
-        def per_piece(name, factor):
-            return [tile("%s%d" % (name, i), [P, factor * (hi - lo)], F32) for i, (lo, hi) in enumerate(PIECES)]
+        V = S // D
+        groups = [slice(0, V // 2), slice(V // 2, V)]
+        sq_pair, sq_cross = tile("sq_pair", [P, 2 * V], F32), tile("sq_cross", [P, V], F32)
+        nc.scalar.activation(warm[:], expo[:, S - 1 : S], ACT.Sqrt, scale=0.0, bias=1.0)
 
-        squares = per_piece("squares", 3)
-        nc.scalar.activation(squares[0][:, 0:4], ratio[:, 0:S:QUARTER], ACT.Sqrt)
+        est = tile("est", [P, S], F32)
+        pair_sum, pair_diff = tile("pair_sum", [P, 2 * V], F32), tile("pair_diff", [P, 2 * V], F32)
+        cross, mean = tile("cross", [P, V], F32), tile("mean", [P, V], F32)
+        inner, variance = tile("inner", [P, V], F32), tile("variance", [P, V], F32)
+        spread, result = tile("spread", [P, V], F32), tile("result", [P, V], F32)
 
-        est, pair_sum, diffs = per_piece("est", 4), per_piece("pair_sum", 2), per_piece("diffs", 3)
-        mean, inner, variance = per_piece("mean", 1), per_piece("inner", 1), per_piece("variance", 1)
-        spread, result = per_piece("spread", 1), per_piece("result", 1)
-        width = [hi - lo for lo, hi in PIECES]
+        def estimate(lo, hi):
+            c = slice(D * lo, D * hi)
+            nc.vector.tensor_tensor(est[:, c], ratio[:, c], vis_sb[:, c], ALU.mult)
 
-        def estimate(i):
-            lo, hi = PIECES[i]
-            nc.vector.tensor_tensor(est[i][:], ratio[:, D * lo : D * hi], vis_sb[:, D * lo : D * hi], ALU.mult)
+        def within_pairs(lo, hi):
+            even, odd = est[:, D * lo : D * hi : 2], est[:, D * lo + 1 : D * hi : 2]
+            nc.vector.tensor_tensor(pair_sum[:, 2 * lo : 2 * hi], even, odd, ALU.add)
+            nc.vector.tensor_tensor(pair_diff[:, 2 * lo : 2 * hi], even, odd, ALU.subtract)
 
-        def within_pairs(i):
-            nc.vector.tensor_tensor(pair_sum[i][:], est[i][:, 0::2], est[i][:, 1::2], ALU.add)
-            nc.vector.tensor_tensor(diffs[i][:, : 2 * width[i]], est[i][:, 0::2], est[i][:, 1::2], ALU.subtract)
+        def first(t, g):
+            return t[:, 2 * g.start : 2 * g.stop : 2]
 
-        def between_pairs(i):
-            nc.vector.tensor_tensor(diffs[i][:, 2 * width[i] :], pair_sum[i][:, 0::2], pair_sum[i][:, 1::2], ALU.subtract)
-            nc.scalar.activation(squares[i][:], diffs[i][:], ACT.Square)
+        def second(t, g):
+            return t[:, 2 * g.start + 1 : 2 * g.stop : 2]
 
-        pieces = range(len(PIECES))
-        estimate(0)
-        for i in pieces:
-            within_pairs(i)
-            if i + 1 in pieces:
-                estimate(i + 1)
-            between_pairs(i)
-        for i in pieces:
-            nc.vector.tensor_tensor(mean[i][:], pair_sum[i][:, 0::2], pair_sum[i][:, 1::2], ALU.add)
-        for i in pieces:
-            n = width[i]
-            nc.vector.tensor_tensor(inner[i][:], squares[i][:, 0 : 2 * n : 2], squares[i][:, 1 : 2 * n : 2], ALU.add)
-            nc.vector.scalar_tensor_tensor(variance[i][:], inner[i][:], 2.0, squares[i][:, 2 * n :], ALU.mult, ALU.add)
-            nc.scalar.activation(spread[i][:], variance[i][:], ACT.Sqrt, bias=0.05)
-        for i, (lo, hi) in enumerate(PIECES):
-            nc.vector.scalar_tensor_tensor(result[i][:], spread[i][:], kap_sb[:, 0:1], mean[i][:], ALU.mult, ALU.add)
-            nc.sync.dma_start(out[:, lo:hi], result[i][:])
+        estimate(*PIECES[0])
+        for i, piece in enumerate(PIECES):
+            if i + 1 < len(PIECES):
+                estimate(*PIECES[i + 1])
+            within_pairs(*piece)
+        for g in groups:
+            pairs = slice(2 * g.start, 2 * g.stop)
+            nc.scalar.activation(sq_pair[:, pairs], pair_diff[:, pairs], ACT.Square)
+        for g in groups:
+            nc.vector.tensor_tensor(cross[:, g], first(pair_sum, g), second(pair_sum, g), ALU.subtract)
+            nc.scalar.activation(sq_cross[:, g], cross[:, g], ACT.Square)
+        nc.vector.tensor_tensor(mean[:], pair_sum[:, 0::2], pair_sum[:, 1::2], ALU.add)
+        for g in groups:
+            nc.vector.tensor_tensor(inner[:, g], first(sq_pair, g), second(sq_pair, g), ALU.add)
+        for g in groups:
+            nc.vector.scalar_tensor_tensor(variance[:, g], inner[:, g], 2.0, sq_cross[:, g], ALU.mult, ALU.add)
+            nc.scalar.activation(spread[:, g], variance[:, g], ACT.Sqrt, bias=0.05)
+        for g in groups:
+            nc.vector.scalar_tensor_tensor(result[:, g], spread[:, g], kap_sb[:, 0:1], mean[:, g], ALU.mult, ALU.add)
+            nc.sync.dma_start(out[:, g], result[:, g])

import math
from contextlib import ExitStack

import concourse.mybir as mybir

K, T, S, D, N = 512, 4096, 1024, 4, 128
FLOPS = 3 * 2 * K * N * S

F32 = mybir.dt.float32
BF16 = mybir.dt.bfloat16
I32 = mybir.dt.int32
U32 = mybir.dt.uint32
U16 = mybir.dt.uint16
U8 = mybir.dt.uint8
FP8X4 = mybir.dt.float8_e4m3fn_x4
ALU = mybir.AluOpType
ACT = mybir.ActivationFunctionType

P = 128
PACK = 4
HALVES = 2
HALF = S // HALVES
QUARTER = S // 4
PIECES = ((0, 64), (64, 128), (128, 256))
FLOOR = 2.0 ** -30
KNEE = math.log(1.0 / FLOOR - 1.0)


def tile_picked_ymisw_bal_p_kernel(tc, x_words, x_scales, w1, w2, w3, vis, kap, offs, out):
    nc = tc.nc
    with ExitStack() as ctx:
        keep = ctx.enter_context(tc.tile_pool(name="keep", bufs=1))
        psum = ctx.enter_context(tc.psum_pool(name="psum", bufs=1))

        def tile(name, shape, dtype, tag=None):
            return keep.tile(shape, dtype, name=name, tag=tag or name, align_bytes=64)

        offsets = keep.tile([P, S // 16], U16, name="offsets")
        nc.sync.dma_start(offsets[:], offs)

        scale_table = tile("scale_table", [P, T], U8)
        nc.vector.memset(scale_table[:].bitcast(I32), 0)

        seed = tile("seed", [P, 1], F32)
        warm = tile("warm", [P, 1], F32)
        nc.vector.memset(seed[:], 0.0)
        nc.scalar.activation(warm[:], seed[:], ACT.Sigmoid)

        planes = tile("planes", [P, S], U8)
        nc.vector.memset(planes[:].bitcast(I32), 0)

        raw = {}

        def load_weight(name, w):
            raw[name] = tile("raw_" + name, [P, PACK, N], F32)
            nc.sync.dma_start(raw[name][:], w.rearrange("(p j) n -> p j n", j=PACK))

        load_weight("p", w2)
        load_weight("q", w3)
        nc.sync.dma_start(scale_table[0:P:8, :].bitcast(I32), x_scales[0].bitcast(I32))
        word_table = tile("word_table", [P, T], I32)
        nc.sync.dma_start(word_table[:], x_words[0].rearrange("p n t -> p (n t)").bitcast(I32))
        load_weight("f", w1)
        kap_sb = tile("kap_sb", [P, 1], F32)
        nc.sync.dma_start(kap_sb[:], kap)

        grouped, codes, scales = {}, {}, {}

        def round_weight(name):
            grouped[name] = tile("grouped_" + name, [P, N * PACK], BF16)
            nc.scalar.copy(
                grouped[name][:].rearrange("p (c i j) -> p c j i", i=4, j=PACK),
                raw[name][:].rearrange("p j (c i) -> p c j i", i=4),
            )

        def quantize_weight(name, tag=None):
            codes[name] = tile("codes_" + name, [P, N], U32, tag)
            scales[name] = tile("scales_" + name, [P, N], U8)
            nc.vector.quantize_mx(out=codes[name][:].bitcast(FP8X4), scales=scales[name][:], in_=grouped[name][:])

        picked_scales = tile("picked_scales", [P, S], U8)
        nc.vector.tensor_copy(picked_scales[:], scale_table[:].indirect(offsets[:]))
        for j in range(4):
            nc.scalar.dma_start(planes[j:P:32, :].bitcast(I32), picked_scales[8 * j : P : 32, :].bitcast(I32))
        vis_sb = tile("vis_sb", [P, S], F32, "picked_scales")
        nc.sync.dma_start(vis_sb[:], vis)
        for name in ("p", "q"):
            round_weight(name)
            quantize_weight(name)
        round_weight("f")

        picked_words = [tile("picked_words%d" % h, [P, HALF], U32) for h in range(HALVES)]
        cols = HALF // 16
        for h in range(HALVES):
            nc.vector.tensor_copy(
                picked_words[h][:],
                word_table[:].bitcast(U32).indirect(offsets[:, h * cols : (h + 1) * cols]),
            )

        halves = [slice(h * HALF, (h + 1) * HALF) for h in range(HALVES)]
        quarters = [slice(a, a + QUARTER) for a in range(0, S, QUARTER)]
        y = {}

        def product(name, c, bank):
            h, lo = divmod(c.start, HALF)
            width = c.stop - c.start
            y[name, c.start] = psum.tile([P, width], F32, name="y_%s%d" % (name, c.start), tag="bank%d" % bank)
            nc.tensor.matmul_mx(
                out=y[name, c.start][:],
                lhsT=codes[name][:].bitcast(FP8X4),
                lhsT_scale=scales[name][:],
                rhs=picked_words[h][:, lo : lo + width].bitcast(FP8X4),
                rhs_scale=planes[:, c],
                start=True,
                stop=True,
            )

        sig = tile("sig", [P, 2 * S], F32)
        sig_p, sig_q = sig[:, :S], sig[:, S:]
        for h in range(HALVES):
            for name, dst, base in (("p", sig_p, 0), ("q", sig_q, 4)):
                for i in (2 * h, 2 * h + 1):
                    c = quarters[i]
                    product(name, c, base + i)
                    nc.scalar.activation(dst[:, c], y[name, c.start][:], ACT.Sigmoid, scale=-1.0)

        log_joint = tile("log_joint", [P, S], F32)
        nc.scalar.activation(warm[:], sig_p[:, S - 1 : S], ACT.Ln)

        over_p, over = tile("over_p", [P, S], F32), tile("over", [P, S], F32)
        floor_q, joint = tile("floor_q", [P, S], F32), tile("joint", [P, S], F32)

        def excess(h):
            for c in quarters[2 * h : 2 * h + 2]:
                nc.vector.tensor_scalar(over_p[:, c], y["p", c.start][:], KNEE, -2.0 * KNEE, ALU.max, ALU.add)
            for c in quarters[2 * h : 2 * h + 2]:
                nc.vector.scalar_tensor_tensor(over[:, c], y["q", c.start][:], KNEE, over_p[:, c], ALU.max, ALU.add)

        def floored_product(h):
            nc.vector.tensor_scalar_max(floor_q[:, halves[h]], sig_q[:, halves[h]], FLOOR)
            nc.vector.scalar_tensor_tensor(
                joint[:, halves[h]], sig_p[:, halves[h]], FLOOR, floor_q[:, halves[h]], ALU.max, ALU.mult
            )

        excess(0)
        floored_product(0)
        floored_product(1)
        excess(1)

        for c in quarters:
            nc.scalar.activation(log_joint[:, c], joint[:, c], ACT.Ln)

        density, log_density = tile("density", [P, S], F32), tile("log_density", [P, S], F32)
        for c in quarters:
            nc.vector.scalar_tensor_tensor(density[:, c], over[:, c], 0.4, log_joint[:, c], ALU.add, ALU.subtract)
            nc.scalar.activation(log_density[:, c], density[:, c], ACT.Ln, scale=float(D))

        quantize_weight("f")
        for h in range(HALVES):
            product("f", halves[h], h)

        ratio = tile("ratio", [P, S], F32)
        nc.scalar.activation(warm[:], log_density[:, HALF : HALF + 1], ACT.Exp)
        expo = tile("expo", [P, S], F32)
        for h in range(HALVES):
            nc.vector.scalar_tensor_tensor(
                expo[:, halves[h]], y["f", h * HALF][:], 0.6, log_density[:, halves[h]], ALU.mult, ALU.subtract
            )
        for lo, hi in PIECES:
            nc.scalar.activation(ratio[:, D * lo : D * hi], expo[:, D * lo : D * hi], ACT.Exp)

        V = S // D
        groups = [slice(0, V // 2), slice(V // 2, V)]
        sq_pair, sq_cross = tile("sq_pair", [P, 2 * V], F32), tile("sq_cross", [P, V], F32)
        nc.scalar.activation(warm[:], expo[:, S - 1 : S], ACT.Sqrt, scale=0.0, bias=1.0)

        est = tile("est", [P, S], F32)
        pair_sum, pair_diff = tile("pair_sum", [P, 2 * V], F32), tile("pair_diff", [P, 2 * V], F32)
        cross, mean = tile("cross", [P, V], F32), tile("mean", [P, V], F32)
        inner, variance = tile("inner", [P, V], F32), tile("variance", [P, V], F32)
        spread, result = tile("spread", [P, V], F32), tile("result", [P, V], F32)

        def estimate(lo, hi):
            c = slice(D * lo, D * hi)
            nc.vector.tensor_tensor(est[:, c], ratio[:, c], vis_sb[:, c], ALU.mult)

        def within_pairs(lo, hi):
            even, odd = est[:, D * lo : D * hi : 2], est[:, D * lo + 1 : D * hi : 2]
            nc.vector.tensor_tensor(pair_sum[:, 2 * lo : 2 * hi], even, odd, ALU.add)
            nc.vector.tensor_tensor(pair_diff[:, 2 * lo : 2 * hi], even, odd, ALU.subtract)

        def first(t, g):
            return t[:, 2 * g.start : 2 * g.stop : 2]

        def second(t, g):
            return t[:, 2 * g.start + 1 : 2 * g.stop : 2]

        estimate(*PIECES[0])
        for i, piece in enumerate(PIECES):
            if i + 1 < len(PIECES):
                estimate(*PIECES[i + 1])
            within_pairs(*piece)
        for g in groups:
            pairs = slice(2 * g.start, 2 * g.stop)
            nc.scalar.activation(sq_pair[:, pairs], pair_diff[:, pairs], ACT.Square)
        for g in groups:
            nc.vector.tensor_tensor(cross[:, g], first(pair_sum, g), second(pair_sum, g), ALU.subtract)
            nc.scalar.activation(sq_cross[:, g], cross[:, g], ACT.Square)
        nc.vector.tensor_tensor(mean[:], pair_sum[:, 0::2], pair_sum[:, 1::2], ALU.add)
        for g in groups:
            nc.vector.tensor_tensor(inner[:, g], first(sq_pair, g), second(sq_pair, g), ALU.add)
        for g in groups:
            nc.vector.scalar_tensor_tensor(variance[:, g], inner[:, g], 2.0, sq_cross[:, g], ALU.mult, ALU.add)
            nc.scalar.activation(spread[:, g], variance[:, g], ACT.Sqrt, bias=0.05)
        for g in groups:
            nc.vector.scalar_tensor_tensor(result[:, g], spread[:, g], kap_sb[:, 0:1], mean[:, g], ALU.mult, ALU.add)
            nc.sync.dma_start(out[:, g], result[:, g])
